import numpy as np
import ml_dtypes


def mxq(x, axis, fmt="e4m3"):
    dtype, down = {"e4m3": (ml_dtypes.float8_e4m3fn, 7), "e5m2": (ml_dtypes.float8_e5m2, 14)}[fmt]
    v = np.moveaxis(np.asarray(x, np.float32).astype(ml_dtypes.bfloat16).astype(np.float64), axis, -1)
    blocks = v.reshape(v.shape[:-1] + (-1, 32))
    amax = np.abs(blocks).max(-1, keepdims=True)
    byte = np.maximum(np.where(amax > 0, np.frexp(amax)[1] - 1 + 127, 0) - down, 1)
    scale = np.exp2(byte - 127.0)
    codes = (blocks / scale).astype(np.float32).astype(dtype).astype(np.float64)
    return np.moveaxis((codes * scale).reshape(v.shape), -1, axis)


WIDE = False


def mx_kscale(k):
    if not WIDE:
        return np.ones(k)
    levels = np.array([10, -10, 5, -5, 0])
    if k % 512:
        return np.exp2(np.random.permutation(np.resize(levels, k // 32))).repeat(32)
    a = np.empty((k // 512, 16))
    for p in range(k // 512):
        a[p, :8] = np.random.permutation(np.resize(levels, 8))
        for g in range(8):
            far = levels[np.abs(levels - a[p, g]) >= 10]
            a[p, g + 8] = far[np.random.randint(len(far))]
    return np.exp2(a.ravel()).repeat(32)


def f64(x):
    return np.asarray(x).astype(np.float64)


def striped(idx):
    return np.tile(idx.reshape(-1, 16).T, (8, 1)).astype(np.uint16)


def unstriped(offs):
    return offs[:16].T.reshape(-1).astype(np.int64)


def pack_weight(w):
    k, n = w.shape
    w = f64(np.asarray(w, np.float32).astype(ml_dtypes.bfloat16)).reshape(k // 32, 32, n)
    amax = np.abs(w).max(1)
    byte = np.clip(np.where(amax > 0, np.frexp(amax)[1] - 1 + 127 - 7, 1), 1, 254)
    scaled = (w * np.exp2(127.0 - byte)[:, None, :]).reshape(k, n).astype(np.float32)
    words = np.ascontiguousarray(scaled.reshape(k // 512, 128, 4, n).transpose(0, 1, 3, 2)).astype(ml_dtypes.float8_e4m3fn).view(np.uint8)
    return words, np.ascontiguousarray(byte.astype(np.uint8).reshape(k // 512, 16, n))


def unpack_weight(words, scales):
    g, p, n, _ = words.shape
    vals = np.ascontiguousarray(words).view(ml_dtypes.float8_e4m3fn).astype(np.float64) * np.repeat(np.exp2(scales.astype(np.float64) - 127.0), 8, axis=1)[..., None]
    return vals.transpose(0, 1, 3, 2).reshape(g * 512, n)


E2M1 = np.array([0.0, 0.5, 1.0, 1.5, 2.0, 3.0, 4.0, 6.0, -0.0, -0.5, -1.0, -1.5, -2.0, -3.0, -4.0, -6.0])


def pack_fp4(w):
    k, n = w.shape
    w = f64(np.asarray(w, np.float32).astype(ml_dtypes.bfloat16)).reshape(k // 32, 32, n)
    amax = np.abs(w).max(1)
    mant, ex = np.frexp(amax / 6.0)
    byte = np.clip(np.where(amax > 0, np.where(mant > 0.5, ex, ex - 1) + 127, 1), 1, 254)
    scaled = (w * np.exp2(127.0 - byte)[:, None, :]).reshape(k, n).astype(np.float32)
    c = np.ascontiguousarray(scaled.reshape(k // 512, 128, 4, n).transpose(0, 1, 3, 2)).astype(ml_dtypes.float4_e2m1fn).view(np.uint8) & 0xF
    words = (c[..., 0::2] | (c[..., 1::2] << 4)).reshape(k // 512, 128, 2 * n)
    return np.ascontiguousarray(words), np.ascontiguousarray(byte.astype(np.uint8).reshape(k // 512, 16, n))


def unpack_fp4(words, scales):
    g, _, n = scales.shape
    words = np.ascontiguousarray(words).reshape(g, 128, n, 2)
    nib = np.empty((g, 128, n, 4), np.uint8)
    nib[..., 0::2] = words & 0xF
    nib[..., 1::2] = words >> 4
    vals = E2M1[nib] * np.repeat(np.exp2(scales.astype(np.float64) - 127.0), 8, axis=1)[..., None]
    return vals.transpose(0, 1, 3, 2).reshape(g * 512, n)


K, T, S, D, N, H, V, U = 1024, 2048, 1024, 4, 128, 512, 256, 512


def setup_inputs():
    n = np.random.standard_normal
    s = mx_kscale(K)[:, None]
    u = mx_kscale(H)
    packed_xT = pack_weight(n((K, T)) * s)
    packed_w1 = pack_fp4(n((K, H)) / np.sqrt(K) / s)
    packed_w2 = pack_fp4(n((K, H)) / np.sqrt(K) / s)
    packed_w3 = pack_fp4(n((H, N)) / np.sqrt(H) / u[:, None])
    return {
        "x_words": packed_xT[0],
        "x_scales": packed_xT[1],
        "w1_words": packed_w1[0],
        "w1_scales": packed_w1[1],
        "w2_words": packed_w2[0],
        "w2_scales": packed_w2[1],
        "qry": (n((H, U))).astype(np.float32),
        "unit": (np.random.uniform(0.6, 1.4, (H, 1)) * u[:, None]).astype(np.float32),
        "w3_words": packed_w3[0],
        "w3_scales": packed_w3[1],
        "offs": striped(np.random.permutation(T)[:S]),
        "b1": striped(np.random.permutation(np.concatenate([np.arange(V), np.random.randint(0, V, U - V)]))),
        "b2": striped(np.random.permutation(np.concatenate([np.arange(V), np.random.randint(0, V, U - V)]))),
        "b3": striped(np.random.permutation(np.concatenate([np.arange(V), np.random.randint(0, V, U - V)]))),
    }


def reference(x_words, x_scales, w1_words, w1_scales, w2_words, w2_scales, qry, unit, w3_words, w3_scales, offs, b1, b2, b3):
    xq = unpack_weight(x_words, x_scales)[:, unstriped(offs)]
    y = unpack_fp4(w1_words, w1_scales).T @ xq
    blk = y.reshape(len(y), -1, D).mean(axis=2)
    e1 = np.exp(np.tanh(blk[:, unstriped(b1)] * f64(qry)))
    yv = unpack_fp4(w2_words, w2_scales).T @ xq
    vblk = yv.reshape(len(yv), -1, D).mean(axis=2)
    e2 = np.exp(np.tanh(blk[:, unstriped(b2)] * f64(qry)))
    e3 = np.exp(np.tanh(blk[:, unstriped(b3)] * f64(qry)))
    num = e1 * vblk[:, unstriped(b1)] + e2 * vblk[:, unstriped(b2)] + e3 * vblk[:, unstriped(b3)]
    den = e1 + e2 + e3
    hid = f64(unit) * (num / den - vblk[:, unstriped(b1)])
    return unpack_fp4(w3_words, w3_scales).T @ mxq(hid, 0, "e4m3")

@@ -1,0 +1,211 @@
+from contextlib import ExitStack
+
+import concourse.mybir as mybir
+from concourse.masks import make_identity
+
+K, T, S, D, N, H, V, U = 1024, 2048, 1024, 4, 128, 512, 256, 512
+FLOPS = 2 * K * H * S * 2 + 2 * H * N * U
+
+F32 = mybir.dt.float32
+BF16 = mybir.dt.bfloat16
+I32 = mybir.dt.int32
+U32 = mybir.dt.uint32
+U16 = mybir.dt.uint16
+U8 = mybir.dt.uint8
+FP8X4 = mybir.dt.float8_e4m3fn_x4
+FP4X4 = mybir.dt.float4_e2m1fn_x4
+ACT = mybir.ActivationFunctionType
+ALU = mybir.AluOpType
+
+P = 128
+PASSES = K // 512
+TILES = H // P
+HALVES = V // P
+QUADS = 4
+WINDOW = 544
+QUERY_PARTS = ((0, 384), (384, 512))
+OUT_PIECES = ((0, 256), (256, 384), (384, 512))
+
+
+def tile_picked_ymoba_diff_p_kernel(
+    tc, x_words, x_scales, w1_words, w1_scales, w2_words, w2_scales, qry, unit, w3_words, w3_scales, offs, b1, b2, b3, out
+):
+    nc = tc.nc
+    with ExitStack() as ctx:
+        keep = ctx.enter_context(tc.tile_pool(name="keep", bufs=1))
+        ring = ctx.enter_context(tc.tile_pool(name="ring", bufs=3))
+        psum = ctx.enter_context(tc.psum_pool(name="psum", bufs=1))
+
+        def bank(b, name):
+            return psum.tile([P, 512], F32, name=name, tag="bank%d" % b)
+
+        offs_sb = keep.tile([P, S // 16], U16, name="offs_sb")
+        xs_all = keep.tile([P, T], U8, name="xs_all", align_bytes=64)
+        xw = [keep.tile([P, T], I32, name="xw%d" % o, tag="xw%d" % o, align_bytes=64) for o in range(PASSES)]
+        w_planes = [keep.tile([P, PASSES, H], U8, name="w_planes%d" % m, align_bytes=64) for m in range(2)]
+        w1_sb = keep.tile([P, PASSES, 2 * H], U8, name="w1_sb", align_bytes=64)
+        w3_sb = keep.tile([P, 2 * N], U8, name="w3_sb", align_bytes=64)
+        w3_plane = keep.tile([P, N], U8, name="w3_plane", align_bytes=64)
+        xs_second = keep.tile([P, S], U8, name="xs_second", align_bytes=64)
+        lists = [keep.tile([P, U // 16], U16, name="list%d" % a) for a in range(3)]
+        unit_sb = keep.tile([P, TILES], F32, name="unit_sb")
+
+        def load_planes(queue, plane, scales):
+            for q in range(QUADS):
+                queue.dma_start(
+                    plane[32 * q : 32 * q + 4, :, :].bitcast(I32),
+                    scales[:, 4 * q : 4 * q + 4, :].rearrange("o j c -> j o c").bitcast(I32),
+                )
+
+        nc.vector.memset(xs_all[:].bitcast(I32), 0)
+        for plane in w_planes:
+            nc.vector.memset(plane[:].rearrange("p o c -> p (o c)").bitcast(I32), 0)
+        nc.vector.memset(w3_plane[:].bitcast(I32), 0)
+        nc.vector.memset(xs_second[:].bitcast(I32), 0)
+
+        nc.sync.dma_start(offs_sb[:], offs)
+        nc.scalar.dma_start(xw[0][:], x_words[0].rearrange("p n t -> p (n t)").bitcast(I32))
+        for q in range(QUADS):
+            nc.sync.dma_start(xs_all[32 * q : 32 * q + 8, :].bitcast(I32), x_scales[:, 4 * q : 4 * q + 4, :].bitcast(I32))
+        load_planes(nc.sync, w_planes[0], w1_scales)
+        nc.sync.dma_start(w1_sb[:].bitcast(I32), w1_words.rearrange("o p c -> p o c").bitcast(I32))
+        nc.sync.dma_start(xw[1][:], x_words[1].rearrange("p n t -> p (n t)").bitcast(I32))
+        for a, picks in enumerate((b1, b2, b3)):
+            nc.sync.dma_start(lists[a][:], picks)
+        with nc.allow_non_contiguous_dma(reason="one value of unit a partition"):
+            nc.gpsimd.dma_start(unit_sb[:], unit.rearrange("(t p) o -> p (t o)", p=P))
+        load_planes(nc.gpsimd, w_planes[1], w2_scales)
+        nc.gpsimd.dma_start(w3_sb[:].bitcast(I32), w3_words[0].bitcast(I32))
+        for q in range(QUADS):
+            nc.gpsimd.dma_start(w3_plane[32 * q : 32 * q + 4, :].bitcast(I32), w3_scales[0, 4 * q : 4 * q + 4, :].bitcast(I32))
+
+        ident = keep.tile([P, P], F32, name="ident")
+        make_identity(nc, ident[:])
+        tables = [[keep.tile([P, WINDOW], F32, name="table%d_%d" % (m, t)) for t in range(TILES)] for m in range(2)]
+        for m in range(2):
+            for t in range(TILES):
+                nc.vector.memset(tables[m][t][:, V:], 0.0)
+        v_scale = keep.tile([P, TILES], F32, name="v_scale")
+        nc.scalar.mul(v_scale[:], unit_sb[:], -0.125)
+
+        xs_picked = keep.tile([P, S], U8, name="xs_picked", tag="xs_picked", align_bytes=64)
+        nc.vector.tensor_copy(xs_picked[:], xs_all[:].indirect(offs_sb[:]))
+        xs_first = keep.tile([P, S], U8, name="xs_first", align_bytes=64)
+        nc.vector.tensor_copy(
+            xs_first[:].rearrange("p (h d v) -> p h d v", h=HALVES, d=D),
+            xs_picked[:].rearrange("p (h v d) -> p h d v", h=HALVES, d=D),
+        )
+        for q in range(QUADS):
+            nc.scalar.dma_start(xs_second[32 * q : 32 * q + 4, :].bitcast(I32), xs_first[32 * q + 4 : 32 * q + 8, :].bitcast(I32))
+        x_planes = (xs_first, xs_second)
+        q_sb = keep.tile([P, TILES, U], F32, name="q_sb", tag="xs_picked", align_bytes=64)
+        nc.sync.dma_start(q_sb[:, 0, :], qry[0:P, :])
+        nc.sync.dma_start(q_sb[:, 1:, :], qry[P:, :].rearrange("(t p) r -> p t r", p=P))
+        xg = [[keep.tile([P, D, P], U32, name="xg%d_%d" % (o, h), align_bytes=64) for h in range(HALVES)] for o in range(PASSES)]
+        for o in range(PASSES):
+            for h in range(HALVES):
+                nc.vector.tensor_copy(
+                    xg[o][h][:].rearrange("p d v -> p v d"),
+                    xw[o][:].bitcast(U32).indirect(offs_sb[:, 32 * h : 32 * (h + 1)]),
+                )
+        w2_sb = keep.tile([P, PASSES, 2 * H], U8, name="w2_sb", tag="xw0", align_bytes=64)
+        nc.sync.dma_start(w2_sb[:].bitcast(I32), w2_words.rearrange("o p c -> p o c").bitcast(I32))
+        w_words = (w1_sb, w2_sb)
+
+        def block_means(m, t):
+            acc = bank(t % 2, "acc")
+            for h in range(HALVES):
+                steps = [(o, d) for o in range(PASSES) for d in range(D)]
+                for n, (o, d) in enumerate(steps):
+                    c = (h * D + d) * P
+                    nc.tensor.matmul_mx(
+                        out=acc[:, h * P : (h + 1) * P],
+                        lhsT=w_words[m][:, o, 2 * t * P : 2 * (t + 1) * P].bitcast(FP4X4),
+                        lhsT_scale=w_planes[m][:, o, t * P : (t + 1) * P],
+                        rhs=xg[o][h][:, d, :].bitcast(FP8X4),
+                        rhs_scale=x_planes[o][:, c : c + P],
+                        start=(n == 0),
+                        stop=(n == len(steps) - 1),
+                    )
+            scale = 1.0 / D if m == 0 else v_scale[:, t : t + 1]
+            nc.scalar.activation(tables[m][t][:, :V], acc[:, :V], ACT.Copy, scale=scale)
+
+        for m in range(2):
+            for t in range(TILES):
+                block_means(m, t)
+
+        den = [bank(2 + rb, "den") for rb in range(U // P)]
+        e = [[keep.tile([P, U], F32, name="e%d_%d" % (t, a)) for a in range(3)] for t in range(TILES)]
+        for t in range(TILES):
+            for a in range(3):
+                g = ring.tile([P, U], F32, name="g")
+                nc.vector.tensor_tensor(g[:], tables[0][t][:].indirect(lists[a][:]), q_sb[:, t, :], ALU.mult)
+                bounded = ring.tile([P, U], F32, name="bounded")
+                nc.scalar.activation(bounded[:], g[:], ACT.Tanh)
+                nc.scalar.activation(e[t][a][:], bounded[:], ACT.Exp)
+            for rb in range(U // P):
+                for a in range(3):
+                    nc.tensor.matmul(
+                        den[rb][:, t * P : (t + 1) * P], e[t][a][:, rb * P : (rb + 1) * P], ident[:],
+                        start=(a == 0), stop=(a == 2), is_transpose=True,
+                    )
+        logs = [keep.tile([P, H], F32, name="log%d" % rb) for rb in range(U // P)]
+        for rb in range(U // P):
+            nc.scalar.activation(logs[rb][:], den[rb][:], ACT.Ln, bias=-1.0)
+        half_tanh = [keep.tile([P, H], F32, name="half_tanh%d" % rb) for rb in range(U // P)]
+        for rb in range(U // P):
+            nc.scalar.activation(half_tanh[rb][:], logs[rb][:], ACT.Tanh, scale=0.5)
+
+        num = [bank((6 + rb) % 8, "num") for rb in range(U // P)]
+        hid_t = [keep.tile([P, H], BF16, name="hid_t%d" % rb) for rb in range(U // P)]
+
+        def values(r0, r1):
+            n = r1 - r0
+            for t in range(TILES):
+                rest = ring.tile([P, n], F32, name="rest")
+                nc.vector.scalar_tensor_tensor(rest[:], e[t][1][:, r0:r1], -1.0, e[t][2][:, r0:r1], ALU.mult, ALU.subtract)
+                factors = (rest[:], e[t][1][:, r0:r1], e[t][2][:, r0:r1])
+                terms = []
+                for a in (1, 2, 0):
+                    term = ring.tile([P, n], F32, name="term%d" % a)
+                    nc.vector.tensor_tensor(term[:], tables[1][t][:].indirect(lists[a][:, r0 // 16 : r1 // 16]), factors[a], ALU.mult)
+                    terms.append(term)
+                for rb in range(r0 // P, r1 // P):
+                    for a in range(3):
+                        c = rb * P - r0
+                        nc.tensor.matmul(
+                            num[rb][:, t * P : (t + 1) * P], terms[a][:, c : c + P], ident[:],
+                            start=(a == 0), stop=(a == 2), is_transpose=True,
+                        )
+
+        def project(i, r0, r1):
+            n = r1 - r0
+            turned = bank(2 + i, "turned")
+            for rb in range(r0 // P, r1 // P):
+                nc.vector.scalar_tensor_tensor(hid_t[rb][:], half_tanh[rb][:], 1.0, num[rb][:], ALU.subtract, ALU.mult)
+                words = hid_t[rb][:].bitcast(F32)
+                for u in range(2):
+                    c = 2 * (rb * P - r0) + u * P
+                    nc.tensor.transpose(turned[:, c : c + P], words[:, u : 2 * P : 2], ident[:])
+            hid = keep.tile([P, 4 * n], BF16, name="hid%d" % i, align_bytes=64)
+            nc.scalar.copy(
+                hid[:].bitcast(F32).rearrange("p (b r u) -> p b r u", r=P, u=2),
+                turned[:, : 2 * n].rearrange("p (b u r) -> p b r u", r=P, u=2),
+            )
+            codes = keep.tile([P, n], U32, name="codes%d" % i, align_bytes=64)
+            plane = keep.tile([P, n], U8, name="plane%d" % i, align_bytes=64)
+            nc.vector.quantize_mx(out=codes[:].bitcast(FP8X4), scales=plane[:], in_=hid[:])
+            acc = bank(5 + i, "projected")
+            nc.tensor.matmul_mx(
+                out=acc[:, :n], lhsT=w3_sb[:].bitcast(FP4X4), lhsT_scale=w3_plane[:],
+                rhs=codes[:].bitcast(FP8X4), rhs_scale=plane[:], start=True, stop=True,
+            )
+            result = keep.tile([P, n], F32, name="result%d" % i)
+            nc.scalar.copy(result[:], acc[:, :n])
+            nc.sync.dma_start(out[:, r0:r1], result[:])
+
+        for r0, r1 in QUERY_PARTS:
+            values(r0, r1)
+            for i, (p0, p1) in enumerate(OUT_PIECES):
+                if r0 <= p0 and p1 <= r1:
+                    project(i, p0, p1)

@@ -43,12 +43,10 @@ def tile_picked_ymoba_diff_p_kernel(
         xs_all = keep.tile([P, T], U8, name="xs_all", align_bytes=64)
         xw = [keep.tile([P, T], I32, name="xw%d" % o, tag="xw%d" % o, align_bytes=64) for o in range(PASSES)]
         w_planes = [keep.tile([P, PASSES, H], U8, name="w_planes%d" % m, align_bytes=64) for m in range(2)]
-        w1_sb = keep.tile([P, PASSES, 2 * H], U8, name="w1_sb", align_bytes=64)
-        w3_sb = keep.tile([P, 2 * N], U8, name="w3_sb", align_bytes=64)
+        w1_sb = keep.tile([P, PASSES, 2 * H], U8, name="w1_sb", tag="w1_sb", align_bytes=64)
         w3_plane = keep.tile([P, N], U8, name="w3_plane", align_bytes=64)
-        xs_second = keep.tile([P, S], U8, name="xs_second", align_bytes=64)
+        xs_first = keep.tile([P, S], U8, name="xs_first", align_bytes=64)
         lists = [keep.tile([P, U // 16], U16, name="list%d" % a) for a in range(3)]
-        unit_sb = keep.tile([P, TILES], F32, name="unit_sb")
 
         def load_planes(queue, plane, scales):
             for q in range(QUADS):
@@ -57,25 +55,25 @@ def tile_picked_ymoba_diff_p_kernel(
                     scales[:, 4 * q : 4 * q + 4, :].rearrange("o j c -> j o c").bitcast(I32),
                 )
 
-        nc.vector.memset(xs_all[:].bitcast(I32), 0)
-        for plane in w_planes:
-            nc.vector.memset(plane[:].rearrange("p o c -> p (o c)").bitcast(I32), 0)
-        nc.vector.memset(w3_plane[:].bitcast(I32), 0)
-        nc.vector.memset(xs_second[:].bitcast(I32), 0)
+        def load_words(o):
+            nc.sync.dma_start(xw[o][:], x_words[o].rearrange("p n t -> p (n t)").bitcast(I32))
 
         nc.sync.dma_start(offs_sb[:], offs)
-        nc.scalar.dma_start(xw[0][:], x_words[0].rearrange("p n t -> p (n t)").bitcast(I32))
-        for q in range(QUADS):
-            nc.sync.dma_start(xs_all[32 * q : 32 * q + 8, :].bitcast(I32), x_scales[:, 4 * q : 4 * q + 4, :].bitcast(I32))
-        load_planes(nc.sync, w_planes[0], w1_scales)
+        scale_rows = x_scales.rearrange("o q c -> (o q) c").bitcast(I32)
+        nc.sync.dma_start(xs_all[100:, :].bitcast(I32), scale_rows[:28, :])
+        nc.sync.dma_start(xs_all[96:100, :].bitcast(I32), scale_rows[28:, :])
+        load_words(0)
         nc.sync.dma_start(w1_sb[:].bitcast(I32), w1_words.rearrange("o p c -> p o c").bitcast(I32))
-        nc.sync.dma_start(xw[1][:], x_words[1].rearrange("p n t -> p (n t)").bitcast(I32))
         for a, picks in enumerate((b1, b2, b3)):
             nc.sync.dma_start(lists[a][:], picks)
-        with nc.allow_non_contiguous_dma(reason="one value of unit a partition"):
-            nc.gpsimd.dma_start(unit_sb[:], unit.rearrange("(t p) o -> p (t o)", p=P))
+        load_words(1)
+        nc.gpsimd.memset(w_planes[0][:].rearrange("p o c -> p (o c)").bitcast(I32), 0)
+        nc.vector.memset(xs_all[:96, :].bitcast(I32), 0)
+        nc.vector.memset(w_planes[1][:].rearrange("p o c -> p (o c)").bitcast(I32), 0)
+        nc.vector.memset(w3_plane[:].bitcast(I32), 0)
+        nc.vector.memset(xs_first[:].bitcast(I32), 0)
+        load_planes(nc.gpsimd, w_planes[0], w1_scales)
         load_planes(nc.gpsimd, w_planes[1], w2_scales)
-        nc.gpsimd.dma_start(w3_sb[:].bitcast(I32), w3_words[0].bitcast(I32))
         for q in range(QUADS):
             nc.gpsimd.dma_start(w3_plane[32 * q : 32 * q + 4, :].bitcast(I32), w3_scales[0, 4 * q : 4 * q + 4, :].bitcast(I32))
 
@@ -85,19 +83,19 @@ def tile_picked_ymoba_diff_p_kernel(
         for m in range(2):
             for t in range(TILES):
                 nc.vector.memset(tables[m][t][:, V:], 0.0)
-        v_scale = keep.tile([P, TILES], F32, name="v_scale")
-        nc.scalar.mul(v_scale[:], unit_sb[:], -0.125)
 
         xs_picked = keep.tile([P, S], U8, name="xs_picked", tag="xs_picked", align_bytes=64)
         nc.vector.tensor_copy(xs_picked[:], xs_all[:].indirect(offs_sb[:]))
-        xs_first = keep.tile([P, S], U8, name="xs_first", align_bytes=64)
+        xs_dealt = keep.tile([P, S], U8, name="xs_dealt", align_bytes=64)
         nc.vector.tensor_copy(
-            xs_first[:].rearrange("p (h d v) -> p h d v", h=HALVES, d=D),
+            xs_dealt[:].rearrange("p (h d v) -> p h d v", h=HALVES, d=D),
             xs_picked[:].rearrange("p (h v d) -> p h d v", h=HALVES, d=D),
         )
-        for q in range(QUADS):
-            nc.scalar.dma_start(xs_second[32 * q : 32 * q + 4, :].bitcast(I32), xs_first[32 * q + 4 : 32 * q + 8, :].bitcast(I32))
-        x_planes = (xs_first, xs_second)
+        x_planes = (xs_first, xs_dealt)
+        for o in range(PASSES):
+            for q in range(QUADS - o):
+                row = 100 + 16 * o + 4 * q
+                nc.scalar.dma_start(x_planes[o][32 * q : 32 * q + 4, :].bitcast(I32), xs_dealt[row : row + 4, :].bitcast(I32))
         q_sb = keep.tile([P, TILES, U], F32, name="q_sb", tag="xs_picked", align_bytes=64)
         nc.sync.dma_start(q_sb[:, 0, :], qry[0:P, :])
         nc.sync.dma_start(q_sb[:, 1:, :], qry[P:, :].rearrange("(t p) r -> p t r", p=P))
@@ -108,37 +106,54 @@ def tile_picked_ymoba_diff_p_kernel(
                     xg[o][h][:].rearrange("p d v -> p v d"),
                     xw[o][:].bitcast(U32).indirect(offs_sb[:, 32 * h : 32 * (h + 1)]),
                 )
-        w2_sb = keep.tile([P, PASSES, 2 * H], U8, name="w2_sb", tag="xw0", align_bytes=64)
+        w2_sb = keep.tile([P, PASSES, 2 * H], U8, name="w2_sb", tag="xw1", align_bytes=64)
         nc.sync.dma_start(w2_sb[:].bitcast(I32), w2_words.rearrange("o p c -> p o c").bitcast(I32))
         w_words = (w1_sb, w2_sb)
+        unit_sb = keep.tile([P, TILES], F32, name="unit_sb", tag="xw0", align_bytes=64)
+        with nc.allow_non_contiguous_dma(reason="one value of unit a partition"):
+            nc.sync.dma_start(unit_sb[:], unit.rearrange("(t p) o -> p (t o)", p=P))
+        v_scale = keep.tile([P, TILES], F32, name="v_scale")
+        nc.scalar.mul(v_scale[:], unit_sb[:], -0.125)
 
-        def block_means(m, t):
-            acc = bank(t % 2, "acc")
+        def add_pass(acc, m, t, h, o):
+            for d in range(D):
+                c = (h * D + d) * P
+                nc.tensor.matmul_mx(
+                    out=acc,
+                    lhsT=w_words[m][:, o, 2 * t * P : 2 * (t + 1) * P].bitcast(FP4X4),
+                    lhsT_scale=w_planes[m][:, o, t * P : (t + 1) * P],
+                    rhs=xg[o][h][:, d, :].bitcast(FP8X4),
+                    rhs_scale=x_planes[o][:, c : c + P],
+                    start=(o == 0 and d == 0),
+                    stop=(o == PASSES - 1 and d == D - 1),
+                )
+
+        first = [bank(6 + h, "first") for h in range(HALVES)]
+        for o in range(PASSES):
             for h in range(HALVES):
-                steps = [(o, d) for o in range(PASSES) for d in range(D)]
-                for n, (o, d) in enumerate(steps):
-                    c = (h * D + d) * P
-                    nc.tensor.matmul_mx(
-                        out=acc[:, h * P : (h + 1) * P],
-                        lhsT=w_words[m][:, o, 2 * t * P : 2 * (t + 1) * P].bitcast(FP4X4),
-                        lhsT_scale=w_planes[m][:, o, t * P : (t + 1) * P],
-                        rhs=xg[o][h][:, d, :].bitcast(FP8X4),
-                        rhs_scale=x_planes[o][:, c : c + P],
-                        start=(n == 0),
-                        stop=(n == len(steps) - 1),
-                    )
-            scale = 1.0 / D if m == 0 else v_scale[:, t : t + 1]
-            nc.scalar.activation(tables[m][t][:, :V], acc[:, :V], ACT.Copy, scale=scale)
-
+                add_pass(first[h][:, :P], 0, 0, h, o)
+        for h in range(HALVES):
+            nc.scalar.activation(tables[0][0][:, h * P : (h + 1) * P], first[h][:, :P], ACT.Copy, scale=1.0 / D)
         for m in range(2):
             for t in range(TILES):
-                block_means(m, t)
+                if (m, t) == (0, 0):
+                    continue
+                acc = bank(t % 2, "acc")
+                for h in range(HALVES):
+                    for o in range(PASSES):
+                        add_pass(acc[:, h * P : (h + 1) * P], m, t, h, o)
+                scale = 1.0 / D if m == 0 else v_scale[:, t : t + 1]
+                nc.scalar.activation(tables[m][t][:, :V], acc[:, :V], ACT.Copy, scale=scale)
+
+        w3_sb = keep.tile([P, 2 * N], U8, name="w3_sb", tag="w1_sb", align_bytes=64)
+        nc.sync.dma_start(w3_sb[:].bitcast(I32), w3_words[0].bitcast(I32))
 
         den = [bank(2 + rb, "den") for rb in range(U // P)]
         e = [[keep.tile([P, U], F32, name="e%d_%d" % (t, a)) for a in range(3)] for t in range(TILES)]
+        rest = [keep.tile([P, U], F32, name="rest%d" % t) for t in range(TILES)]
         for t in range(TILES):
             for a in range(3):
-                g = ring.tile([P, U], F32, name="g")
+                g = ring.tile([P, U], F32, name="g", bufs=12)
                 nc.vector.tensor_tensor(g[:], tables[0][t][:].indirect(lists[a][:]), q_sb[:, t, :], ALU.mult)
                 bounded = ring.tile([P, U], F32, name="bounded")
                 nc.scalar.activation(bounded[:], g[:], ACT.Tanh)
@@ -149,34 +164,47 @@ def tile_picked_ymoba_diff_p_kernel(
                         den[rb][:, t * P : (t + 1) * P], e[t][a][:, rb * P : (rb + 1) * P], ident[:],
                         start=(a == 0), stop=(a == 2), is_transpose=True,
                     )
+            summed = bank(6, "summed")
+            for rb in range(U // P):
+                for a in (1, 2):
+                    nc.tensor.matmul(
+                        summed[:, rb * P : (rb + 1) * P], e[t][a][:, rb * P : (rb + 1) * P], ident[:],
+                        start=(a == 1), stop=(a == 2), is_transpose=True,
+                    )
+            summed_sb = ring.tile([P, U], F32, name="summed_sb")
+            nc.scalar.copy(summed_sb[:], summed[:])
+            back = bank(6, "back")
+            for rb in range(U // P):
+                nc.tensor.transpose(back[:, rb * P : (rb + 1) * P], summed_sb[:, rb * P : (rb + 1) * P], ident[:])
+            nc.scalar.activation(rest[t][:], back[:], ACT.Copy, scale=-1.0)
         logs = [keep.tile([P, H], F32, name="log%d" % rb) for rb in range(U // P)]
         for rb in range(U // P):
             nc.scalar.activation(logs[rb][:], den[rb][:], ACT.Ln, bias=-1.0)
-        half_tanh = [keep.tile([P, H], F32, name="half_tanh%d" % rb) for rb in range(U // P)]
+        half_tanh = [keep.tile([P, H], F32, name="half_tanh%d" % rb, tag="half_tanh%d" % rb) for rb in range(U // P)]
         for rb in range(U // P):
             nc.scalar.activation(half_tanh[rb][:], logs[rb][:], ACT.Tanh, scale=0.5)
 
-        num = [bank((6 + rb) % 8, "num") for rb in range(U // P)]
+        num = [bank(b, "num") for b in (0, 1, 7, 6)]
         hid_t = [keep.tile([P, H], BF16, name="hid_t%d" % rb) for rb in range(U // P)]
 
-        def values(r0, r1):
+        def values(r0, r1, t, first_tag=None):
             n = r1 - r0
-            for t in range(TILES):
-                rest = ring.tile([P, n], F32, name="rest")
-                nc.vector.scalar_tensor_tensor(rest[:], e[t][1][:, r0:r1], -1.0, e[t][2][:, r0:r1], ALU.mult, ALU.subtract)
-                factors = (rest[:], e[t][1][:, r0:r1], e[t][2][:, r0:r1])
-                terms = []
-                for a in (1, 2, 0):
+            factors = (rest[t], e[t][1], e[t][2])
+            terms = []
+            for a in (1, 2, 0):
+                if first_tag and a == 1:
+                    term = keep.tile([P, n], F32, name="term", tag=first_tag)
+                else:
                     term = ring.tile([P, n], F32, name="term%d" % a)
-                    nc.vector.tensor_tensor(term[:], tables[1][t][:].indirect(lists[a][:, r0 // 16 : r1 // 16]), factors[a], ALU.mult)
-                    terms.append(term)
-                for rb in range(r0 // P, r1 // P):
-                    for a in range(3):
-                        c = rb * P - r0
-                        nc.tensor.matmul(
-                            num[rb][:, t * P : (t + 1) * P], terms[a][:, c : c + P], ident[:],
-                            start=(a == 0), stop=(a == 2), is_transpose=True,
-                        )
+                nc.vector.tensor_tensor(term[:], tables[1][t][:].indirect(lists[a][:, r0 // 16 : r1 // 16]), factors[a][:, r0:r1], ALU.mult)
+                terms.append(term)
+            for rb in range(r0 // P, r1 // P):
+                for a in range(3):
+                    c = rb * P - r0
+                    nc.tensor.matmul(
+                        num[rb][:, t * P : (t + 1) * P], terms[a][:, c : c + P], ident[:],
+                        start=(a == 0), stop=(a == 2), is_transpose=True,
+                    )
 
         def project(i, r0, r1):
             n = r1 - r0
@@ -188,24 +216,29 @@ def tile_picked_ymoba_diff_p_kernel(
                     c = 2 * (rb * P - r0) + u * P
                     nc.tensor.transpose(turned[:, c : c + P], words[:, u : 2 * P : 2], ident[:])
             hid = keep.tile([P, 4 * n], BF16, name="hid%d" % i, align_bytes=64)
-            nc.scalar.copy(
+            move = nc.vector.tensor_copy if r1 == U else nc.scalar.copy
+            move(
                 hid[:].bitcast(F32).rearrange("p (b r u) -> p b r u", r=P, u=2),
                 turned[:, : 2 * n].rearrange("p (b u r) -> p b r u", r=P, u=2),
             )
             codes = keep.tile([P, n], U32, name="codes%d" % i, align_bytes=64)
             plane = keep.tile([P, n], U8, name="plane%d" % i, align_bytes=64)
             nc.vector.quantize_mx(out=codes[:].bitcast(FP8X4), scales=plane[:], in_=hid[:])
-            acc = bank(5 + i, "projected")
+            acc = bank((5, 0, 1)[i], "projected")
             nc.tensor.matmul_mx(
                 out=acc[:, :n], lhsT=w3_sb[:].bitcast(FP4X4), lhsT_scale=w3_plane[:],
                 rhs=codes[:].bitcast(FP8X4), rhs_scale=plane[:], start=True, stop=True,
             )
             result = keep.tile([P, n], F32, name="result%d" % i)
-            nc.scalar.copy(result[:], acc[:, :n])
+            move(result[:], acc[:, :n])
             nc.sync.dma_start(out[:, r0:r1], result[:])
 
-        for r0, r1 in QUERY_PARTS:
-            values(r0, r1)
-            for i, (p0, p1) in enumerate(OUT_PIECES):
-                if r0 <= p0 and p1 <= r1:
-                    project(i, p0, p1)
+        for t in range(TILES):
+            values(0, 384, t)
+        values(384, 512, 0)
+        values(384, 512, 1)
+        project(0, 0, 256)
+        values(384, 512, 2, "half_tanh1")
+        values(384, 512, 3)
+        project(1, 256, 384)
+        project(2, 384, 512)

@@ -4,7 +4,7 @@ import concourse.mybir as mybir
 from concourse.masks import make_identity
 
 K, T, S, D, N, H, V, U = 1024, 2048, 1024, 4, 128, 512, 256, 512
-FLOPS = 2 * K * H * S * 2 + 2 * H * N * U
+FLOPS = 2 * (2 * K * H * S) + 2 * H * N * U
 
 F32 = mybir.dt.float32
 BF16 = mybir.dt.bfloat16
@@ -21,10 +21,13 @@ P = 128
 PASSES = K // 512
 TILES = H // P
 HALVES = V // P
+GROUPS = U // P
 QUADS = 4
-WINDOW = 544
-QUERY_PARTS = ((0, 384), (384, 512))
-OUT_PIECES = ((0, 256), (256, 384), (384, 512))
+LISTS = 3
+PER_COLUMN = 16
+WINDOW = U + 32
+PARKED = 100
+LAST = U - P
 
 
 def tile_picked_ymoba_diff_p_kernel(
@@ -39,18 +42,21 @@ def tile_picked_ymoba_diff_p_kernel(
         def bank(b, name):
             return psum.tile([P, 512], F32, name=name, tag="bank%d" % b)
 
-        offs_sb = keep.tile([P, S // 16], U16, name="offs_sb")
+        def add_turned(dst, src, first, last):
+            nc.tensor.matmul(dst, src, ident[:], start=first, stop=last, is_transpose=True)
+
+        offs_sb = keep.tile([P, S // PER_COLUMN], U16, name="offs_sb")
         xs_all = keep.tile([P, T], U8, name="xs_all", align_bytes=64)
         xw = [keep.tile([P, T], I32, name="xw%d" % o, tag="xw%d" % o, align_bytes=64) for o in range(PASSES)]
         w_planes = [keep.tile([P, PASSES, H], U8, name="w_planes%d" % m, align_bytes=64) for m in range(2)]
         w1_sb = keep.tile([P, PASSES, 2 * H], U8, name="w1_sb", tag="w1_sb", align_bytes=64)
         w3_plane = keep.tile([P, N], U8, name="w3_plane", align_bytes=64)
         xs_first = keep.tile([P, S], U8, name="xs_first", align_bytes=64)
-        lists = [keep.tile([P, U // 16], U16, name="list%d" % a) for a in range(3)]
+        lists = [keep.tile([P, U // PER_COLUMN], U16, name="list%d" % a) for a in range(LISTS)]
 
-        def load_planes(queue, plane, scales):
+        def load_planes(plane, scales):
             for q in range(QUADS):
-                queue.dma_start(
+                nc.gpsimd.dma_start(
                     plane[32 * q : 32 * q + 4, :, :].bitcast(I32),
                     scales[:, 4 * q : 4 * q + 4, :].rearrange("o j c -> j o c").bitcast(I32),
                 )
@@ -60,8 +66,8 @@ def tile_picked_ymoba_diff_p_kernel(
 
         nc.sync.dma_start(offs_sb[:], offs)
         scale_rows = x_scales.rearrange("o q c -> (o q) c").bitcast(I32)
-        nc.sync.dma_start(xs_all[100:, :].bitcast(I32), scale_rows[:28, :])
-        nc.sync.dma_start(xs_all[96:100, :].bitcast(I32), scale_rows[28:, :])
+        nc.sync.dma_start(xs_all[PARKED:, :].bitcast(I32), scale_rows[: P - PARKED, :])
+        nc.sync.dma_start(xs_all[96:PARKED, :].bitcast(I32), scale_rows[P - PARKED :, :])
         load_words(0)
         nc.sync.dma_start(w1_sb[:].bitcast(I32), w1_words.rearrange("o p c -> p o c").bitcast(I32))
         for a, picks in enumerate((b1, b2, b3)):
@@ -72,8 +78,8 @@ def tile_picked_ymoba_diff_p_kernel(
         nc.vector.memset(w_planes[1][:].rearrange("p o c -> p (o c)").bitcast(I32), 0)
         nc.vector.memset(w3_plane[:].bitcast(I32), 0)
         nc.vector.memset(xs_first[:].bitcast(I32), 0)
-        load_planes(nc.gpsimd, w_planes[0], w1_scales)
-        load_planes(nc.gpsimd, w_planes[1], w2_scales)
+        load_planes(w_planes[0], w1_scales)
+        load_planes(w_planes[1], w2_scales)
         for q in range(QUADS):
             nc.gpsimd.dma_start(w3_plane[32 * q : 32 * q + 4, :].bitcast(I32), w3_scales[0, 4 * q : 4 * q + 4, :].bitcast(I32))
 
@@ -94,17 +100,18 @@ def tile_picked_ymoba_diff_p_kernel(
         x_planes = (xs_first, xs_dealt)
         for o in range(PASSES):
             for q in range(QUADS - o):
-                row = 100 + 16 * o + 4 * q
+                row = PARKED + 16 * o + 4 * q
                 nc.scalar.dma_start(x_planes[o][32 * q : 32 * q + 4, :].bitcast(I32), xs_dealt[row : row + 4, :].bitcast(I32))
         q_sb = keep.tile([P, TILES, U], F32, name="q_sb", tag="xs_picked", align_bytes=64)
         nc.sync.dma_start(q_sb[:, 0, :], qry[0:P, :])
         nc.sync.dma_start(q_sb[:, 1:, :], qry[P:, :].rearrange("(t p) r -> p t r", p=P))
         xg = [[keep.tile([P, D, P], U32, name="xg%d_%d" % (o, h), align_bytes=64) for h in range(HALVES)] for o in range(PASSES)]
+        half_columns = D * P // PER_COLUMN
         for o in range(PASSES):
             for h in range(HALVES):
                 nc.vector.tensor_copy(
                     xg[o][h][:].rearrange("p d v -> p v d"),
-                    xw[o][:].bitcast(U32).indirect(offs_sb[:, 32 * h : 32 * (h + 1)]),
+                    xw[o][:].bitcast(U32).indirect(offs_sb[:, half_columns * h : half_columns * (h + 1)]),
                 )
         w2_sb = keep.tile([P, PASSES, 2 * H], U8, name="w2_sb", tag="xw1", align_bytes=64)
         nc.sync.dma_start(w2_sb[:].bitcast(I32), w2_words.rearrange("o p c -> p o c").bitcast(I32))
@@ -112,8 +119,6 @@ def tile_picked_ymoba_diff_p_kernel(
         unit_sb = keep.tile([P, TILES], F32, name="unit_sb", tag="xw0", align_bytes=64)
         with nc.allow_non_contiguous_dma(reason="one value of unit a partition"):
             nc.sync.dma_start(unit_sb[:], unit.rearrange("(t p) o -> p (t o)", p=P))
-        v_scale = keep.tile([P, TILES], F32, name="v_scale")
-        nc.scalar.mul(v_scale[:], unit_sb[:], -0.125)
 
         def add_pass(acc, m, t, h, o):
             for d in range(D):
@@ -134,111 +139,120 @@ def tile_picked_ymoba_diff_p_kernel(
                 add_pass(first[h][:, :P], 0, 0, h, o)
         for h in range(HALVES):
             nc.scalar.activation(tables[0][0][:, h * P : (h + 1) * P], first[h][:, :P], ACT.Copy, scale=1.0 / D)
-        for m in range(2):
-            for t in range(TILES):
-                if (m, t) == (0, 0):
-                    continue
-                acc = bank(t % 2, "acc")
-                for h in range(HALVES):
-                    for o in range(PASSES):
-                        add_pass(acc[:, h * P : (h + 1) * P], m, t, h, o)
-                scale = 1.0 / D if m == 0 else v_scale[:, t : t + 1]
-                nc.scalar.activation(tables[m][t][:, :V], acc[:, :V], ACT.Copy, scale=scale)
+        others = [(m, t) for m in range(2) for t in range(TILES)][1:]
+        for n, (m, t) in enumerate(others):
+            acc = bank((0, 1, 7)[n % 3], "acc")
+            for h in range(HALVES):
+                for o in range(PASSES):
+                    add_pass(acc[:, h * P : (h + 1) * P], m, t, h, o)
+            scale = 1.0 / D if m == 0 else unit_sb[:, t : t + 1]
+            nc.scalar.activation(tables[m][t][:, :V], acc[:, :V], ACT.Copy, scale=scale)
 
         w3_sb = keep.tile([P, 2 * N], U8, name="w3_sb", tag="w1_sb", align_bytes=64)
         nc.sync.dma_start(w3_sb[:].bitcast(I32), w3_words[0].bitcast(I32))
 
-        den = [bank(2 + rb, "den") for rb in range(U // P)]
-        e = [[keep.tile([P, U], F32, name="e%d_%d" % (t, a)) for a in range(3)] for t in range(TILES)]
+        den = [bank(2 + r, "den") for r in range(GROUPS)]
+        e = [[keep.tile([P, U], F32, name="e%d_%d" % (t, a)) for a in range(LISTS)] for t in range(TILES)]
         rest = [keep.tile([P, U], F32, name="rest%d" % t) for t in range(TILES)]
         for t in range(TILES):
-            for a in range(3):
-                g = ring.tile([P, U], F32, name="g", bufs=12)
+            for a in range(LISTS):
+                g = ring.tile([P, U], F32, name="g", bufs=TILES * LISTS)
                 nc.vector.tensor_tensor(g[:], tables[0][t][:].indirect(lists[a][:]), q_sb[:, t, :], ALU.mult)
                 bounded = ring.tile([P, U], F32, name="bounded")
                 nc.scalar.activation(bounded[:], g[:], ACT.Tanh)
                 nc.scalar.activation(e[t][a][:], bounded[:], ACT.Exp)
-            for rb in range(U // P):
-                for a in range(3):
-                    nc.tensor.matmul(
-                        den[rb][:, t * P : (t + 1) * P], e[t][a][:, rb * P : (rb + 1) * P], ident[:],
-                        start=(a == 0), stop=(a == 2), is_transpose=True,
-                    )
-            summed = bank(6, "summed")
-            for rb in range(U // P):
-                for a in (1, 2):
-                    nc.tensor.matmul(
-                        summed[:, rb * P : (rb + 1) * P], e[t][a][:, rb * P : (rb + 1) * P], ident[:],
-                        start=(a == 1), stop=(a == 2), is_transpose=True,
-                    )
+            if t == 0:
+                summed = []
+            elif t < TILES - 1:
+                summed = [(bank(6, "summed"), range(GROUPS))]
+            else:
+                summed = [(bank(b, "summed"), groups) for b, groups in ((0, (0,)), (1, (1,)), (7, (2, 3)))]
+            for part, groups in summed:
+                for r in groups:
+                    for a in (1, 2):
+                        add_turned(part[:, r * P : (r + 1) * P], e[t][a][:, r * P : (r + 1) * P], a == 1, a == 2)
+            for a in range(LISTS):
+                for r in range(GROUPS):
+                    add_turned(den[r][:, t * P : (t + 1) * P], e[t][a][:, r * P : (r + 1) * P], a == 0, a == LISTS - 1)
+            if t == 0:
+                continue
             summed_sb = ring.tile([P, U], F32, name="summed_sb")
-            nc.scalar.copy(summed_sb[:], summed[:])
+            for part, groups in summed:
+                cols = slice(groups[0] * P, (groups[-1] + 1) * P)
+                nc.scalar.copy(summed_sb[:, cols], part[:, cols])
             back = bank(6, "back")
-            for rb in range(U // P):
-                nc.tensor.transpose(back[:, rb * P : (rb + 1) * P], summed_sb[:, rb * P : (rb + 1) * P], ident[:])
+            for r in range(GROUPS):
+                nc.tensor.transpose(back[:, r * P : (r + 1) * P], summed_sb[:, r * P : (r + 1) * P], ident[:])
             nc.scalar.activation(rest[t][:], back[:], ACT.Copy, scale=-1.0)
-        logs = [keep.tile([P, H], F32, name="log%d" % rb) for rb in range(U // P)]
-        for rb in range(U // P):
-            nc.scalar.activation(logs[rb][:], den[rb][:], ACT.Ln, bias=-1.0)
-        half_tanh = [keep.tile([P, H], F32, name="half_tanh%d" % rb, tag="half_tanh%d" % rb) for rb in range(U // P)]
-        for rb in range(U // P):
-            nc.scalar.activation(half_tanh[rb][:], logs[rb][:], ACT.Tanh, scale=0.5)
+
+        def paired(tile):
+            return tile[:].rearrange("p (u m j) -> p u m j", u=2, j=2)
+
+        def paired_from_bank(tile):
+            return tile[:].rearrange("p (m u j) -> p u m j", u=2, j=2)
+
+        logs = [keep.tile([P, H], F32, name="log%d" % r) for r in range(GROUPS)]
+        for r in range(GROUPS):
+            nc.scalar.activation(paired(logs[r]), paired_from_bank(den[r]), ACT.Ln, bias=-1.0, scale=float(D))
+        recip = [keep.tile([P, H], F32, name="recip%d" % r, tag="recip%d" % r) for r in range(GROUPS)]
+        for r in range(GROUPS):
+            nc.scalar.activation(recip[r][:], logs[r][:], ACT.Sigmoid, scale=-1.0)
 
         num = [bank(b, "num") for b in (0, 1, 7, 6)]
-        hid_t = [keep.tile([P, H], BF16, name="hid_t%d" % rb) for rb in range(U // P)]
+        hid_turned = [keep.tile([P, H], BF16, name="hid_turned%d" % r) for r in range(GROUPS)]
 
         def values(r0, r1, t, first_tag=None):
-            n = r1 - r0
             factors = (rest[t], e[t][1], e[t][2])
             terms = []
             for a in (1, 2, 0):
                 if first_tag and a == 1:
-                    term = keep.tile([P, n], F32, name="term", tag=first_tag)
+                    term = keep.tile([P, r1 - r0], F32, name="term", tag=first_tag)
                 else:
-                    term = ring.tile([P, n], F32, name="term%d" % a)
-                nc.vector.tensor_tensor(term[:], tables[1][t][:].indirect(lists[a][:, r0 // 16 : r1 // 16]), factors[a][:, r0:r1], ALU.mult)
+                    term = ring.tile([P, r1 - r0], F32, name="term%d" % a, bufs=TILES + 1)
+                picks = lists[a][:, r0 // PER_COLUMN : r1 // PER_COLUMN]
+                nc.vector.tensor_tensor(term[:], tables[1][t][:].indirect(picks), factors[a][:, r0:r1], ALU.mult)
                 terms.append(term)
-            for rb in range(r0 // P, r1 // P):
-                for a in range(3):
-                    c = rb * P - r0
-                    nc.tensor.matmul(
-                        num[rb][:, t * P : (t + 1) * P], terms[a][:, c : c + P], ident[:],
-                        start=(a == 0), stop=(a == 2), is_transpose=True,
-                    )
+            for n, term in enumerate(terms):
+                for r in range(r0 // P, r1 // P):
+                    c = r * P - r0
+                    add_turned(num[r][:, t * P : (t + 1) * P], term[:, c : c + P], n == 0, n == LISTS - 1)
 
         def project(i, r0, r1):
-            n = r1 - r0
-            turned = bank(2 + i, "turned")
-            for rb in range(r0 // P, r1 // P):
-                nc.vector.scalar_tensor_tensor(hid_t[rb][:], half_tanh[rb][:], 1.0, num[rb][:], ALU.subtract, ALU.mult)
-                words = hid_t[rb][:].bitcast(F32)
+            width = r1 - r0
+            turned_back = bank(2 + i, "turned_back")
+            shares = ((0, 1), (1, 2)) if r0 == LAST else ((0, 2),)
+            move = nc.vector.tensor_copy if r0 == LAST else nc.scalar.copy
+            for r in range(r0 // P, r1 // P):
+                for u0, u1 in shares:
+                    nc.vector.tensor_tensor(
+                        paired(hid_turned[r])[:, u0:u1], paired_from_bank(num[r])[:, u0:u1], paired(recip[r])[:, u0:u1], ALU.mult
+                    )
+                words = hid_turned[r][:].bitcast(F32)
                 for u in range(2):
-                    c = 2 * (rb * P - r0) + u * P
-                    nc.tensor.transpose(turned[:, c : c + P], words[:, u : 2 * P : 2], ident[:])
-            hid = keep.tile([P, 4 * n], BF16, name="hid%d" % i, align_bytes=64)
-            move = nc.vector.tensor_copy if r1 == U else nc.scalar.copy
+                    c = 2 * (r * P - r0) + u * P
+                    nc.tensor.transpose(turned_back[:, c : c + P], words[:, u * P : (u + 1) * P], ident[:])
+            hid = keep.tile([P, 4 * width], BF16, name="hid%d" % i, align_bytes=64)
             move(
-                hid[:].bitcast(F32).rearrange("p (b r u) -> p b r u", r=P, u=2),
-                turned[:, : 2 * n].rearrange("p (b u r) -> p b r u", r=P, u=2),
+                hid[:].bitcast(F32).rearrange("p (b c u) -> p b c u", c=P, u=2),
+                turned_back[:, : 2 * width].rearrange("p (b u c) -> p b c u", c=P, u=2),
             )
-            codes = keep.tile([P, n], U32, name="codes%d" % i, align_bytes=64)
-            plane = keep.tile([P, n], U8, name="plane%d" % i, align_bytes=64)
+            codes = keep.tile([P, width], U32, name="codes%d" % i, align_bytes=64)
+            plane = keep.tile([P, width], U8, name="plane%d" % i, align_bytes=64)
             nc.vector.quantize_mx(out=codes[:].bitcast(FP8X4), scales=plane[:], in_=hid[:])
-            acc = bank((5, 0, 1)[i], "projected")
+            projected = bank((5, 0, 1)[i], "projected")
             nc.tensor.matmul_mx(
-                out=acc[:, :n], lhsT=w3_sb[:].bitcast(FP4X4), lhsT_scale=w3_plane[:],
+                out=projected[:, :width], lhsT=w3_sb[:].bitcast(FP4X4), lhsT_scale=w3_plane[:],
                 rhs=codes[:].bitcast(FP8X4), rhs_scale=plane[:], start=True, stop=True,
             )
-            result = keep.tile([P, n], F32, name="result%d" % i)
-            move(result[:], acc[:, :n])
+            result = keep.tile([P, width], F32, name="result%d" % i)
+            move(result[:], projected[:, :width])
             nc.sync.dma_start(out[:, r0:r1], result[:])
 
-        for t in range(TILES):
-            values(0, 384, t)
-        values(384, 512, 0)
-        values(384, 512, 1)
-        project(0, 0, 256)
-        values(384, 512, 2, "half_tanh1")
-        values(384, 512, 3)
-        project(1, 256, 384)
-        project(2, 384, 512)
+        nc.vector.scalar_tensor_tensor(rest[0][:], e[0][1][:], -1.0, e[0][2][:], ALU.mult, ALU.subtract)
+        for t in range(TILES - 1):
+            values(0, U, t)
+        values(0, LAST, TILES - 1)
+        project(0, 0, 2 * P)
+        values(LAST, U, TILES - 1, "recip1")
+        project(1, 2 * P, LAST)
+        project(2, LAST, U)

from contextlib import ExitStack

import concourse.mybir as mybir
from concourse.masks import make_identity

K, T, S, D, N, H, V, U = 1024, 2048, 1024, 4, 128, 512, 256, 512
FLOPS = 2 * (2 * K * H * S) + 2 * H * N * U

F32 = mybir.dt.float32
BF16 = mybir.dt.bfloat16
I32 = mybir.dt.int32
U32 = mybir.dt.uint32
U16 = mybir.dt.uint16
U8 = mybir.dt.uint8
FP8X4 = mybir.dt.float8_e4m3fn_x4
FP4X4 = mybir.dt.float4_e2m1fn_x4
ACT = mybir.ActivationFunctionType
ALU = mybir.AluOpType

P = 128
PASSES = K // 512
TILES = H // P
HALVES = V // P
GROUPS = U // P
QUADS = 4
LISTS = 3
PER_COLUMN = 16
WINDOW = U + 32
PARKED = 100
LAST = U - P


def tile_picked_ymoba_diff_p_kernel(
    tc, x_words, x_scales, w1_words, w1_scales, w2_words, w2_scales, qry, unit, w3_words, w3_scales, offs, b1, b2, b3, out
):
    nc = tc.nc
    with ExitStack() as ctx:
        keep = ctx.enter_context(tc.tile_pool(name="keep", bufs=1))
        ring = ctx.enter_context(tc.tile_pool(name="ring", bufs=3))
        psum = ctx.enter_context(tc.psum_pool(name="psum", bufs=1))

        def bank(b, name):
            return psum.tile([P, 512], F32, name=name, tag="bank%d" % b)

        def add_turned(dst, src, first, last):
            nc.tensor.matmul(dst, src, ident[:], start=first, stop=last, is_transpose=True)

        offs_sb = keep.tile([P, S // PER_COLUMN], U16, name="offs_sb")
        xs_all = keep.tile([P, T], U8, name="xs_all", align_bytes=64)
        xw = [keep.tile([P, T], I32, name="xw%d" % o, tag="xw%d" % o, align_bytes=64) for o in range(PASSES)]
        w_planes = [keep.tile([P, PASSES, H], U8, name="w_planes%d" % m, align_bytes=64) for m in range(2)]
        w1_sb = keep.tile([P, PASSES, 2 * H], U8, name="w1_sb", tag="w1_sb", align_bytes=64)
        w3_plane = keep.tile([P, N], U8, name="w3_plane", align_bytes=64)
        xs_first = keep.tile([P, S], U8, name="xs_first", align_bytes=64)
        lists = [keep.tile([P, U // PER_COLUMN], U16, name="list%d" % a) for a in range(LISTS)]

        def load_planes(plane, scales):
            for q in range(QUADS):
                nc.gpsimd.dma_start(
                    plane[32 * q : 32 * q + 4, :, :].bitcast(I32),
                    scales[:, 4 * q : 4 * q + 4, :].rearrange("o j c -> j o c").bitcast(I32),
                )

        def load_words(o):
            nc.sync.dma_start(xw[o][:], x_words[o].rearrange("p n t -> p (n t)").bitcast(I32))

        nc.sync.dma_start(offs_sb[:], offs)
        scale_rows = x_scales.rearrange("o q c -> (o q) c").bitcast(I32)
        nc.sync.dma_start(xs_all[PARKED:, :].bitcast(I32), scale_rows[: P - PARKED, :])
        nc.sync.dma_start(xs_all[96:PARKED, :].bitcast(I32), scale_rows[P - PARKED :, :])
        load_words(0)
        nc.sync.dma_start(w1_sb[:].bitcast(I32), w1_words.rearrange("o p c -> p o c").bitcast(I32))
        for a, picks in enumerate((b1, b2, b3)):
            nc.sync.dma_start(lists[a][:], picks)
        load_words(1)
        nc.gpsimd.memset(w_planes[0][:].rearrange("p o c -> p (o c)").bitcast(I32), 0)
        nc.vector.memset(xs_all[:96, :].bitcast(I32), 0)
        nc.vector.memset(w_planes[1][:].rearrange("p o c -> p (o c)").bitcast(I32), 0)
        nc.vector.memset(w3_plane[:].bitcast(I32), 0)
        nc.vector.memset(xs_first[:].bitcast(I32), 0)
        load_planes(w_planes[0], w1_scales)
        load_planes(w_planes[1], w2_scales)
        for q in range(QUADS):
            nc.gpsimd.dma_start(w3_plane[32 * q : 32 * q + 4, :].bitcast(I32), w3_scales[0, 4 * q : 4 * q + 4, :].bitcast(I32))

        ident = keep.tile([P, P], F32, name="ident")
        make_identity(nc, ident[:])
        tables = [[keep.tile([P, WINDOW], F32, name="table%d_%d" % (m, t)) for t in range(TILES)] for m in range(2)]
        for m in range(2):
            for t in range(TILES):
                nc.vector.memset(tables[m][t][:, V:], 0.0)

        xs_picked = keep.tile([P, S], U8, name="xs_picked", tag="xs_picked", align_bytes=64)
        nc.vector.tensor_copy(xs_picked[:], xs_all[:].indirect(offs_sb[:]))
        xs_dealt = keep.tile([P, S], U8, name="xs_dealt", align_bytes=64)
        nc.vector.tensor_copy(
            xs_dealt[:].rearrange("p (h d v) -> p h d v", h=HALVES, d=D),
            xs_picked[:].rearrange("p (h v d) -> p h d v", h=HALVES, d=D),
        )
        x_planes = (xs_first, xs_dealt)
        for o in range(PASSES):
            for q in range(QUADS - o):
                row = PARKED + 16 * o + 4 * q
                nc.scalar.dma_start(x_planes[o][32 * q : 32 * q + 4, :].bitcast(I32), xs_dealt[row : row + 4, :].bitcast(I32))
        q_sb = keep.tile([P, TILES, U], F32, name="q_sb", tag="xs_picked", align_bytes=64)
        nc.sync.dma_start(q_sb[:, 0, :], qry[0:P, :])
        nc.sync.dma_start(q_sb[:, 1:, :], qry[P:, :].rearrange("(t p) r -> p t r", p=P))
        xg = [[keep.tile([P, D, P], U32, name="xg%d_%d" % (o, h), align_bytes=64) for h in range(HALVES)] for o in range(PASSES)]
        half_columns = D * P // PER_COLUMN
        for o in range(PASSES):
            for h in range(HALVES):
                nc.vector.tensor_copy(
                    xg[o][h][:].rearrange("p d v -> p v d"),
                    xw[o][:].bitcast(U32).indirect(offs_sb[:, half_columns * h : half_columns * (h + 1)]),
                )
        w2_sb = keep.tile([P, PASSES, 2 * H], U8, name="w2_sb", tag="xw1", align_bytes=64)
        nc.sync.dma_start(w2_sb[:].bitcast(I32), w2_words.rearrange("o p c -> p o c").bitcast(I32))
        w_words = (w1_sb, w2_sb)
        unit_sb = keep.tile([P, TILES], F32, name="unit_sb", tag="xw0", align_bytes=64)
        with nc.allow_non_contiguous_dma(reason="one value of unit a partition"):
            nc.sync.dma_start(unit_sb[:], unit.rearrange("(t p) o -> p (t o)", p=P))

        def add_pass(acc, m, t, h, o):
            for d in range(D):
                c = (h * D + d) * P
                nc.tensor.matmul_mx(
                    out=acc,
                    lhsT=w_words[m][:, o, 2 * t * P : 2 * (t + 1) * P].bitcast(FP4X4),
                    lhsT_scale=w_planes[m][:, o, t * P : (t + 1) * P],
                    rhs=xg[o][h][:, d, :].bitcast(FP8X4),
                    rhs_scale=x_planes[o][:, c : c + P],
                    start=(o == 0 and d == 0),
                    stop=(o == PASSES - 1 and d == D - 1),
                )

        first = [bank(6 + h, "first") for h in range(HALVES)]
        for o in range(PASSES):
            for h in range(HALVES):
                add_pass(first[h][:, :P], 0, 0, h, o)
        for h in range(HALVES):
            nc.scalar.activation(tables[0][0][:, h * P : (h + 1) * P], first[h][:, :P], ACT.Copy, scale=1.0 / D)
        others = [(m, t) for m in range(2) for t in range(TILES)][1:]
        for n, (m, t) in enumerate(others):
            acc = bank((0, 1, 7)[n % 3], "acc")
            for h in range(HALVES):
                for o in range(PASSES):
                    add_pass(acc[:, h * P : (h + 1) * P], m, t, h, o)
            scale = 1.0 / D if m == 0 else unit_sb[:, t : t + 1]
            nc.scalar.activation(tables[m][t][:, :V], acc[:, :V], ACT.Copy, scale=scale)

        w3_sb = keep.tile([P, 2 * N], U8, name="w3_sb", tag="w1_sb", align_bytes=64)
        nc.sync.dma_start(w3_sb[:].bitcast(I32), w3_words[0].bitcast(I32))

        den = [bank(2 + r, "den") for r in range(GROUPS)]
        e = [[keep.tile([P, U], F32, name="e%d_%d" % (t, a)) for a in range(LISTS)] for t in range(TILES)]
        rest = [keep.tile([P, U], F32, name="rest%d" % t) for t in range(TILES)]
        for t in range(TILES):
            for a in range(LISTS):
                g = ring.tile([P, U], F32, name="g", bufs=TILES * LISTS)
                nc.vector.tensor_tensor(g[:], tables[0][t][:].indirect(lists[a][:]), q_sb[:, t, :], ALU.mult)
                bounded = ring.tile([P, U], F32, name="bounded")
                nc.scalar.activation(bounded[:], g[:], ACT.Tanh)
                nc.scalar.activation(e[t][a][:], bounded[:], ACT.Exp)
            if t == 0:
                summed = []
            elif t < TILES - 1:
                summed = [(bank(6, "summed"), range(GROUPS))]
            else:
                summed = [(bank(b, "summed"), groups) for b, groups in ((0, (0,)), (1, (1,)), (7, (2, 3)))]
            for part, groups in summed:
                for r in groups:
                    for a in (1, 2):
                        add_turned(part[:, r * P : (r + 1) * P], e[t][a][:, r * P : (r + 1) * P], a == 1, a == 2)
            for a in range(LISTS):
                for r in range(GROUPS):
                    add_turned(den[r][:, t * P : (t + 1) * P], e[t][a][:, r * P : (r + 1) * P], a == 0, a == LISTS - 1)
            if t == 0:
                continue
            summed_sb = ring.tile([P, U], F32, name="summed_sb")
            for part, groups in summed:
                cols = slice(groups[0] * P, (groups[-1] + 1) * P)
                nc.scalar.copy(summed_sb[:, cols], part[:, cols])
            back = bank(6, "back")
            for r in range(GROUPS):
                nc.tensor.transpose(back[:, r * P : (r + 1) * P], summed_sb[:, r * P : (r + 1) * P], ident[:])
            nc.scalar.activation(rest[t][:], back[:], ACT.Copy, scale=-1.0)

        def paired(tile):
            return tile[:].rearrange("p (u m j) -> p u m j", u=2, j=2)

        def paired_from_bank(tile):
            return tile[:].rearrange("p (m u j) -> p u m j", u=2, j=2)

        logs = [keep.tile([P, H], F32, name="log%d" % r) for r in range(GROUPS)]
        for r in range(GROUPS):
            nc.scalar.activation(paired(logs[r]), paired_from_bank(den[r]), ACT.Ln, bias=-1.0, scale=float(D))
        recip = [keep.tile([P, H], F32, name="recip%d" % r, tag="recip%d" % r) for r in range(GROUPS)]
        for r in range(GROUPS):
            nc.scalar.activation(recip[r][:], logs[r][:], ACT.Sigmoid, scale=-1.0)

        num = [bank(b, "num") for b in (0, 1, 7, 6)]
        hid_turned = [keep.tile([P, H], BF16, name="hid_turned%d" % r) for r in range(GROUPS)]

        def values(r0, r1, t, first_tag=None):
            factors = (rest[t], e[t][1], e[t][2])
            terms = []
            for a in (1, 2, 0):
                if first_tag and a == 1:
                    term = keep.tile([P, r1 - r0], F32, name="term", tag=first_tag)
                else:
                    term = ring.tile([P, r1 - r0], F32, name="term%d" % a, bufs=TILES + 1)
                picks = lists[a][:, r0 // PER_COLUMN : r1 // PER_COLUMN]
                nc.vector.tensor_tensor(term[:], tables[1][t][:].indirect(picks), factors[a][:, r0:r1], ALU.mult)
                terms.append(term)
            for n, term in enumerate(terms):
                for r in range(r0 // P, r1 // P):
                    c = r * P - r0
                    add_turned(num[r][:, t * P : (t + 1) * P], term[:, c : c + P], n == 0, n == LISTS - 1)

        def project(i, r0, r1):
            width = r1 - r0
            turned_back = bank(2 + i, "turned_back")
            shares = ((0, 1), (1, 2)) if r0 == LAST else ((0, 2),)
            move = nc.vector.tensor_copy if r0 == LAST else nc.scalar.copy
            for r in range(r0 // P, r1 // P):
                for u0, u1 in shares:
                    nc.vector.tensor_tensor(
                        paired(hid_turned[r])[:, u0:u1], paired_from_bank(num[r])[:, u0:u1], paired(recip[r])[:, u0:u1], ALU.mult
                    )
                words = hid_turned[r][:].bitcast(F32)
                for u in range(2):
                    c = 2 * (r * P - r0) + u * P
                    nc.tensor.transpose(turned_back[:, c : c + P], words[:, u * P : (u + 1) * P], ident[:])
            hid = keep.tile([P, 4 * width], BF16, name="hid%d" % i, align_bytes=64)
            move(
                hid[:].bitcast(F32).rearrange("p (b c u) -> p b c u", c=P, u=2),
                turned_back[:, : 2 * width].rearrange("p (b u c) -> p b c u", c=P, u=2),
            )
            codes = keep.tile([P, width], U32, name="codes%d" % i, align_bytes=64)
            plane = keep.tile([P, width], U8, name="plane%d" % i, align_bytes=64)
            nc.vector.quantize_mx(out=codes[:].bitcast(FP8X4), scales=plane[:], in_=hid[:])
            projected = bank((5, 0, 1)[i], "projected")
            nc.tensor.matmul_mx(
                out=projected[:, :width], lhsT=w3_sb[:].bitcast(FP4X4), lhsT_scale=w3_plane[:],
                rhs=codes[:].bitcast(FP8X4), rhs_scale=plane[:], start=True, stop=True,
            )
            result = keep.tile([P, width], F32, name="result%d" % i)
            move(result[:], projected[:, :width])
            nc.sync.dma_start(out[:, r0:r1], result[:])

        nc.vector.scalar_tensor_tensor(rest[0][:], e[0][1][:], -1.0, e[0][2][:], ALU.mult, ALU.subtract)
        for t in range(TILES - 1):
            values(0, U, t)
        values(0, LAST, TILES - 1)
        project(0, 0, 2 * P)
        values(LAST, U, TILES - 1, "recip1")
        project(1, 2 * P, LAST)
        project(2, LAST, U)
